import numpy as np
import ml_dtypes


def mxq(x, axis, fmt="e4m3"):
    dtype, down = {"e4m3": (ml_dtypes.float8_e4m3fn, 7), "e5m2": (ml_dtypes.float8_e5m2, 14)}[fmt]
    v = np.moveaxis(np.asarray(x, np.float32).astype(ml_dtypes.bfloat16).astype(np.float64), axis, -1)
    blocks = v.reshape(v.shape[:-1] + (-1, 32))
    amax = np.abs(blocks).max(-1, keepdims=True)
    byte = np.maximum(np.where(amax > 0, np.frexp(amax)[1] - 1 + 127, 0) - down, 1)
    scale = np.exp2(byte - 127.0)
    codes = (blocks / scale).astype(np.float32).astype(dtype).astype(np.float64)
    return np.moveaxis((codes * scale).reshape(v.shape), -1, axis)


WIDE = False


def mx_kscale(k, group=512):
    if not WIDE:
        return np.ones(k)
    levels = np.array([10, -10, 5, -5, 0])
    if group != 512:
        return np.exp2(np.random.permutation(np.resize(levels, k // group))).repeat(group)
    if k % 512:
        return np.exp2(np.random.permutation(np.resize(levels, k // 32))).repeat(32)
    a = np.empty((k // 512, 16))
    for p in range(k // 512):
        a[p, :8] = np.random.permutation(np.resize(levels, 8))
        for g in range(8):
            far = levels[np.abs(levels - a[p, g]) >= 10]
            a[p, g + 8] = far[np.random.randint(len(far))]
    return np.exp2(a.ravel()).repeat(32)


def f64(x):
    return np.asarray(x).astype(np.float64)


E2M1 = np.array([0.0, 0.5, 1.0, 1.5, 2.0, 3.0, 4.0, 6.0, -0.0, -0.5, -1.0, -1.5, -2.0, -3.0, -4.0, -6.0])


def pack_group(w):
    k, n = w.shape
    w = f64(np.asarray(w, np.float32).astype(ml_dtypes.bfloat16)).reshape(k // 32, 32, n)
    amax = np.abs(w).max(1)
    mant, ex = np.frexp(amax / 6.0)
    byte = np.clip(np.where(amax > 0, np.where(mant > 0.5, ex, ex - 1) + 127, 1), 1, 254)
    scaled = (w * np.exp2(127.0 - byte)[:, None, :]).reshape(k, n).astype(np.float32)
    c = np.ascontiguousarray(scaled.reshape(k // 4, 4, n).transpose(0, 2, 1)).astype(ml_dtypes.float4_e2m1fn).view(np.uint8) & 0xF
    return np.ascontiguousarray((c[..., 0::2] | (c[..., 1::2] << 4)).reshape(k // 4, 2 * n)), byte.astype(np.uint8)


def unpack_group(words, scales):
    p, n = words.shape[0], scales.shape[1]
    words = np.ascontiguousarray(words).reshape(p, n, 2)
    nib = np.empty((p, n, 4), np.uint8)
    nib[..., 0::2] = words & 0xF
    nib[..., 1::2] = words >> 4
    return E2M1[nib].transpose(0, 2, 1).reshape(4 * p, n) * np.repeat(np.exp2(scales.astype(np.float64) - 127.0), 32, axis=0)


G, D, M, N = 2, 256, 128, 512


def setup_inputs():
    n = np.random.standard_normal
    s = mx_kscale(D, 0)[:, None]
    w_ = [pack_group(w) for w in n((G, D, M)) / np.sqrt(D) / s]
    u_ = [pack_group(w) for w in n((G, D, M)) / np.sqrt(D) / s]
    return {
        "x": (n((G, D, N)) * s).astype(np.float32),
        "w_words": np.stack([w[0] for w in w_]),
        "w_scales": np.stack([w[1] for w in w_]),
        "u_words": np.stack([w[0] for w in u_]),
        "u_scales": np.stack([w[1] for w in u_]),
    }


def reference(x, w_words, w_scales, u_words, u_scales):
    xq = mxq(f64(x), 1, "e4m3")
    h = np.stack([unpack_group(w_words[g], w_scales[g]) for g in range(G)]).transpose(0, 2, 1) @ xq
    g = np.stack([unpack_group(u_words[g], u_scales[g]) for g in range(G)]).transpose(0, 2, 1) @ xq
    y = np.tanh(h) * g
    return y

@@ -1,0 +1,106 @@
+from contextlib import ExitStack
+
+import concourse.mybir as mybir
+
+G, D, M, N = 2, 256, 128, 512
+FLOPS = 2 * 2 * G * D * M * N
+
+F32 = mybir.dt.float32
+BF16 = mybir.dt.bfloat16
+I32 = mybir.dt.int32
+U32 = mybir.dt.uint32
+U8 = mybir.dt.uint8
+FP8X4 = mybir.dt.float8_e4m3fn_x4
+FP4X4 = mybir.dt.float4_e2m1fn_x4
+ACT = mybir.ActivationFunctionType
+ALU = mybir.AluOpType
+
+P = 128
+PACK = 4
+ROWS = D // PACK
+QUAD = 32
+SCALE_ROWS = 4
+CHUNK = 256
+VEC_COLS = 160
+HALF = N // 2
+
+
+def tile_rows_gglu_tanh_kernel(tc, x, w_words, w_scales, u_words, u_scales, out):
+    nc = tc.nc
+    with ExitStack() as ctx:
+        sb = ctx.enter_context(tc.tile_pool(name="sb", bufs=1))
+        ps = ctx.enter_context(tc.psum_pool(name="ps", bufs=1))
+        ctx.enter_context(tc.manual_schedule())
+
+        w_sb = sb.tile([P, 2 * M], U8, name="w_sb", align_bytes=64)
+        u_sb = sb.tile([P, 2 * M], U8, name="u_sb", align_bytes=64)
+        wscale = sb.tile([P, 2 * M], U8, name="wscale", align_bytes=64)
+        warm_in = sb.tile([P, 1], F32, name="warm_in")
+        warm_out = sb.tile([P, 1], F32, name="warm_out")
+        codes = sb.tile([P, N], U32, name="codes", align_bytes=64)
+        xscale = sb.tile([P, N], U8, name="xscale", align_bytes=64)
+
+        nc.vector.memset(wscale[:].bitcast(I32), 0)
+        nc.vector.memset(warm_in[:], 0.0)
+
+        x_rows = x.rearrange("g (p j) n -> (g p) j n", j=PACK)
+        w_rows = w_scales.rearrange("g f m -> (g f) m").bitcast(I32)
+        u_rows = u_scales.rearrange("g f m -> (g f) m").bitcast(I32)
+
+        def load_scales(engine, rows, col0, quad):
+            engine.dma_start(
+                out=wscale[QUAD * quad : QUAD * quad + SCALE_ROWS, col0 : col0 + M].bitcast(I32),
+                in_=rows[SCALE_ROWS * quad : SCALE_ROWS * (quad + 1), :],
+            )
+
+        nc.scalar.dma_start(out=w_sb[:].bitcast(I32), in_=w_words.rearrange("g p b -> (g p) b").bitcast(I32))
+        nc.sync.dma_start(out=u_sb[:].bitcast(I32), in_=u_words.rearrange("g p b -> (g p) b").bitcast(I32))
+        raw = []
+        for c in range(N // CHUNK):
+            raw_c = sb.tile([P, PACK, CHUNK], F32, name="raw%d" % c)
+            nc.sync.dma_start(out=raw_c[:], in_=x_rows[:, :, c * CHUNK : (c + 1) * CHUNK])
+            raw.append(raw_c)
+        for quad in range(4):
+            load_scales(nc.scalar, w_rows, 0, quad)
+        for quad in (0, 1):
+            load_scales(nc.sync, u_rows, M, quad)
+        for quad in (2, 3):
+            load_scales(nc.gpsimd, u_rows, M, quad)
+        nc.scalar.activation(out=warm_out[:], in_=warm_in[:], func=ACT.Tanh)
+
+        for c in range(N // CHUNK):
+            grouped = sb.tile([P, CHUNK, PACK], BF16, name="grouped%d" % c, align_bytes=64)
+            src = raw[c][:].rearrange("p j (c i) -> p c j i", i=4)
+            dst = grouped[:].rearrange("p (c i) j -> p c j i", i=4)
+            split = VEC_COLS // 4
+            nc.vector.tensor_copy(out=dst[:, :split], in_=src[:, :split])
+            nc.scalar.copy(out=dst[:, split:], in_=src[:, split:])
+            cols = slice(c * CHUNK, (c + 1) * CHUNK)
+            nc.vector.quantize_mx(
+                out=codes[:, cols].bitcast(FP8X4),
+                scales=xscale[:, cols],
+                in_=grouped[:].rearrange("p n j -> p (n j)"),
+            )
+
+        for g in range(G):
+            rows = slice(ROWS * g, ROWS * (g + 1))
+            sums = []
+            for name, words, col0 in (("h", w_sb, 0), ("u", u_sb, M)):
+                acc = ps.tile([M, N], F32, name="acc_%s%d" % (name, g))
+                nc.tensor.matmul_mx(
+                    out=acc[:],
+                    lhsT=words[rows, :].bitcast(FP4X4),
+                    lhsT_scale=wscale[rows, col0 : col0 + M],
+                    rhs=codes[rows, :].bitcast(FP8X4),
+                    rhs_scale=xscale[rows, :],
+                    start=True,
+                    stop=True,
+                )
+                sums.append(acc)
+            for h in range(2):
+                cols = slice(h * HALF, (h + 1) * HALF)
+                gate = sb.tile([M, HALF], F32, name="gate%d_%d" % (g, h))
+                nc.scalar.activation(out=gate[:], in_=sums[0][:, cols], func=ACT.Tanh)
+                result = sb.tile([M, HALF], F32, name="result%d_%d" % (g, h))
+                nc.vector.tensor_tensor(out=result[:], in0=sums[1][:, cols], in1=gate[:], op=ALU.mult)
+                nc.sync.dma_start(out=out[g][:, cols], in_=result[:])

@@ -20,8 +20,7 @@ PACK = 4
 ROWS = D // PACK
 QUAD = 32
 SCALE_ROWS = 4
-CHUNK = 256
-VEC_COLS = 160
+VEC_COLS = 64
 HALF = N // 2
 
 
@@ -35,13 +34,10 @@ def tile_rows_gglu_tanh_kernel(tc, x, w_words, w_scales, u_words, u_scales, out)
         w_sb = sb.tile([P, 2 * M], U8, name="w_sb", align_bytes=64)
         u_sb = sb.tile([P, 2 * M], U8, name="u_sb", align_bytes=64)
         wscale = sb.tile([P, 2 * M], U8, name="wscale", align_bytes=64)
-        warm_in = sb.tile([P, 1], F32, name="warm_in")
-        warm_out = sb.tile([P, 1], F32, name="warm_out")
         codes = sb.tile([P, N], U32, name="codes", align_bytes=64)
         xscale = sb.tile([P, N], U8, name="xscale", align_bytes=64)
 
         nc.vector.memset(wscale[:].bitcast(I32), 0)
-        nc.vector.memset(warm_in[:], 0.0)
 
         x_rows = x.rearrange("g (p j) n -> (g p) j n", j=PACK)
         w_rows = w_scales.rearrange("g f m -> (g f) m").bitcast(I32)
@@ -53,29 +49,31 @@ def tile_rows_gglu_tanh_kernel(tc, x, w_words, w_scales, u_words, u_scales, out)
                 in_=rows[SCALE_ROWS * quad : SCALE_ROWS * (quad + 1), :],
             )
 
+        raw = sb.tile([P, PACK, N], F32, name="raw")
+        nc.sync.dma_start(out=raw[:], in_=x_rows)
         nc.scalar.dma_start(out=w_sb[:].bitcast(I32), in_=w_words.rearrange("g p b -> (g p) b").bitcast(I32))
-        nc.sync.dma_start(out=u_sb[:].bitcast(I32), in_=u_words.rearrange("g p b -> (g p) b").bitcast(I32))
-        raw = []
-        for c in range(N // CHUNK):
-            raw_c = sb.tile([P, PACK, CHUNK], F32, name="raw%d" % c)
-            nc.sync.dma_start(out=raw_c[:], in_=x_rows[:, :, c * CHUNK : (c + 1) * CHUNK])
-            raw.append(raw_c)
-        for quad in range(4):
-            load_scales(nc.scalar, w_rows, 0, quad)
-        for quad in (0, 1):
-            load_scales(nc.sync, u_rows, M, quad)
-        for quad in (2, 3):
-            load_scales(nc.gpsimd, u_rows, M, quad)
-        nc.scalar.activation(out=warm_out[:], in_=warm_in[:], func=ACT.Tanh)
+        nc.scalar.dma_start(out=u_sb[:].bitcast(I32), in_=u_words.rearrange("g p b -> (g p) b").bitcast(I32))
+        for g in range(G):
+            for rows, col0 in ((w_rows, 0), (u_rows, M)):
+                for quad in (2 * g, 2 * g + 1):
+                    load_scales(nc.sync, rows, col0, quad)
 
-        for c in range(N // CHUNK):
-            grouped = sb.tile([P, CHUNK, PACK], BF16, name="grouped%d" % c, align_bytes=64)
-            src = raw[c][:].rearrange("p j (c i) -> p c j i", i=4)
-            dst = grouped[:].rearrange("p (c i) j -> p c j i", i=4)
-            split = VEC_COLS // 4
-            nc.vector.tensor_copy(out=dst[:, :split], in_=src[:, :split])
-            nc.scalar.copy(out=dst[:, split:], in_=src[:, split:])
-            cols = slice(c * CHUNK, (c + 1) * CHUNK)
+        first = sb.tile([P, HALF, PACK], BF16, name="first", align_bytes=64)
+        second = sb.tile([P, HALF, PACK], BF16, name="second", align_bytes=64)
+
+        def walk(grouped, col0, lo, hi):
+            src = raw[:, :, col0 + lo : col0 + hi].rearrange("p j (c i) -> p c j i", i=4)
+            dst = grouped[:, lo:hi, :].rearrange("p (c i) j -> p c j i", i=4)
+            return dst, src
+
+        dst, src = walk(first, 0, 0, HALF)
+        nc.vector.tensor_copy(out=dst, in_=src)
+        dst, src = walk(second, HALF, 0, VEC_COLS)
+        nc.vector.tensor_copy(out=dst, in_=src)
+        dst, src = walk(second, HALF, VEC_COLS, HALF)
+        nc.scalar.activation(out=dst, in_=src, func=ACT.Copy)
+        for c, grouped in enumerate((first, second)):
+            cols = slice(c * HALF, (c + 1) * HALF)
             nc.vector.quantize_mx(
                 out=codes[:, cols].bitcast(FP8X4),
                 scales=xscale[:, cols],

@@ -20,7 +20,7 @@ PACK = 4
 ROWS = D // PACK
 QUAD = 32
 SCALE_ROWS = 4
-VEC_COLS = 64
+VEC_COLS = 56
 HALF = N // 2
 
 
@@ -51,10 +51,10 @@ def tile_rows_gglu_tanh_kernel(tc, x, w_words, w_scales, u_words, u_scales, out)
 
         raw = sb.tile([P, PACK, N], F32, name="raw")
         nc.sync.dma_start(out=raw[:], in_=x_rows)
-        nc.scalar.dma_start(out=w_sb[:].bitcast(I32), in_=w_words.rearrange("g p b -> (g p) b").bitcast(I32))
-        nc.scalar.dma_start(out=u_sb[:].bitcast(I32), in_=u_words.rearrange("g p b -> (g p) b").bitcast(I32))
         for g in range(G):
-            for rows, col0 in ((w_rows, 0), (u_rows, M)):
+            for words, tile_sb, rows, col0 in ((w_words, w_sb, w_rows, 0), (u_words, u_sb, u_rows, M)):
+                if g == 0:
+                    nc.sync.dma_start(out=tile_sb[:].bitcast(I32), in_=words.rearrange("g p b -> (g p) b").bitcast(I32))
                 for quad in (2 * g, 2 * g + 1):
                     load_scales(nc.sync, rows, col0, quad)
 
@@ -62,8 +62,8 @@ def tile_rows_gglu_tanh_kernel(tc, x, w_words, w_scales, u_words, u_scales, out)
         second = sb.tile([P, HALF, PACK], BF16, name="second", align_bytes=64)
 
         def walk(grouped, col0, lo, hi):
-            src = raw[:, :, col0 + lo : col0 + hi].rearrange("p j (c i) -> p c j i", i=4)
-            dst = grouped[:, lo:hi, :].rearrange("p (c i) j -> p c j i", i=4)
+            src = raw[:, :, col0 + lo : col0 + hi].rearrange("p j (c i) -> p c j i", i=2)
+            dst = grouped[:, lo:hi, :].rearrange("p (c i) j -> p c j i", i=2)
             return dst, src
 
         dst, src = walk(first, 0, 0, HALF)

@@ -20,8 +20,10 @@ PACK = 4
 ROWS = D // PACK
 QUAD = 32
 SCALE_ROWS = 4
-VEC_COLS = 56
+VEC_COLS = 48
 HALF = N // 2
+PAIR = PACK // 2
+QUADS = P // QUAD
 
 
 def tile_rows_gglu_tanh_kernel(tc, x, w_words, w_scales, u_words, u_scales, out):
@@ -50,28 +52,30 @@ def tile_rows_gglu_tanh_kernel(tc, x, w_words, w_scales, u_words, u_scales, out)
             )
 
         raw = sb.tile([P, PACK, N], F32, name="raw")
-        nc.sync.dma_start(out=raw[:], in_=x_rows)
-        for g in range(G):
-            for words, tile_sb, rows, col0 in ((w_words, w_sb, w_rows, 0), (u_words, u_sb, u_rows, M)):
-                if g == 0:
-                    nc.sync.dma_start(out=tile_sb[:].bitcast(I32), in_=words.rearrange("g p b -> (g p) b").bitcast(I32))
-                for quad in (2 * g, 2 * g + 1):
-                    load_scales(nc.sync, rows, col0, quad)
+        nc.sync.dma_start(out=raw[:, :PAIR, :], in_=x_rows[:, :PAIR, :])
+        for quad in range(QUADS):
+            load_scales((nc.sync, nc.scalar)[quad % 2], w_rows, 0, quad)
+        nc.sync.dma_start(out=raw[:, PAIR:, :], in_=x_rows[:, PAIR:, :])
+        for words, tile_sb in ((w_words, w_sb), (u_words, u_sb)):
+            nc.sync.dma_start(out=tile_sb[:].bitcast(I32), in_=words.rearrange("g p b -> (g p) b").bitcast(I32))
+        for quad in range(QUADS):
+            load_scales(nc.sync, u_rows, M, quad)
 
         first = sb.tile([P, HALF, PACK], BF16, name="first", align_bytes=64)
         second = sb.tile([P, HALF, PACK], BF16, name="second", align_bytes=64)
 
-        def walk(grouped, col0, lo, hi):
-            src = raw[:, :, col0 + lo : col0 + hi].rearrange("p j (c i) -> p c j i", i=2)
-            dst = grouped[:, lo:hi, :].rearrange("p (c i) j -> p c j i", i=2)
+        def walk(grouped, col0, lo, hi, places):
+            src = raw[:, places, col0 + lo : col0 + hi].rearrange("p j (c i) -> p c j i", i=2)
+            dst = grouped[:, lo:hi, places].rearrange("p (c i) j -> p c j i", i=2)
             return dst, src
 
-        dst, src = walk(first, 0, 0, HALF)
-        nc.vector.tensor_copy(out=dst, in_=src)
-        dst, src = walk(second, HALF, 0, VEC_COLS)
-        nc.vector.tensor_copy(out=dst, in_=src)
-        dst, src = walk(second, HALF, VEC_COLS, HALF)
-        nc.scalar.activation(out=dst, in_=src, func=ACT.Copy)
+        for places in (slice(0, PAIR), slice(PAIR, PACK)):
+            dst, src = walk(second, HALF, VEC_COLS, HALF, places)
+            nc.scalar.activation(out=dst, in_=src, func=ACT.Copy)
+            dst, src = walk(first, 0, 0, HALF, places)
+            nc.vector.tensor_copy(out=dst, in_=src)
+            dst, src = walk(second, HALF, 0, VEC_COLS, places)
+            nc.vector.tensor_copy(out=dst, in_=src)
         for c, grouped in enumerate((first, second)):
             cols = slice(c * HALF, (c + 1) * HALF)
             nc.vector.quantize_mx(
@@ -80,10 +84,10 @@ def tile_rows_gglu_tanh_kernel(tc, x, w_words, w_scales, u_words, u_scales, out)
                 in_=grouped[:].rearrange("p n j -> p (n j)"),
             )
 
-        for g in range(G):
-            rows = slice(ROWS * g, ROWS * (g + 1))
-            sums = []
-            for name, words, col0 in (("h", w_sb, 0), ("u", u_sb, M)):
+        sums = {}
+        for name, words, col0 in (("h", w_sb, 0), ("u", u_sb, M)):
+            for g in range(G):
+                rows = slice(ROWS * g, ROWS * (g + 1))
                 acc = ps.tile([M, N], F32, name="acc_%s%d" % (name, g))
                 nc.tensor.matmul_mx(
                     out=acc[:],
@@ -94,11 +98,13 @@ def tile_rows_gglu_tanh_kernel(tc, x, w_words, w_scales, u_words, u_scales, out)
                     start=True,
                     stop=True,
                 )
-                sums.append(acc)
+                sums[name, g] = acc
+
+        for g in range(G):
             for h in range(2):
                 cols = slice(h * HALF, (h + 1) * HALF)
                 gate = sb.tile([M, HALF], F32, name="gate%d_%d" % (g, h))
-                nc.scalar.activation(out=gate[:], in_=sums[0][:, cols], func=ACT.Tanh)
+                nc.scalar.activation(out=gate[:], in_=sums["h", g][:, cols], func=ACT.Tanh)
                 result = sb.tile([M, HALF], F32, name="result%d_%d" % (g, h))
-                nc.vector.tensor_tensor(out=result[:], in0=sums[1][:, cols], in1=gate[:], op=ALU.mult)
+                nc.vector.tensor_tensor(out=result[:], in0=sums["u", g][:, cols], in1=gate[:], op=ALU.mult)
                 nc.sync.dma_start(out=out[g][:, cols], in_=result[:])

from contextlib import ExitStack

import concourse.mybir as mybir

G, D, M, N = 2, 256, 128, 512
FLOPS = 2 * 2 * G * D * M * N

F32 = mybir.dt.float32
BF16 = mybir.dt.bfloat16
I32 = mybir.dt.int32
U32 = mybir.dt.uint32
U8 = mybir.dt.uint8
FP8X4 = mybir.dt.float8_e4m3fn_x4
FP4X4 = mybir.dt.float4_e2m1fn_x4
ACT = mybir.ActivationFunctionType
ALU = mybir.AluOpType

P = 128
PACK = 4
ROWS = D // PACK
QUAD = 32
SCALE_ROWS = 4
VEC_COLS = 48
HALF = N // 2
PAIR = PACK // 2
QUADS = P // QUAD


def tile_rows_gglu_tanh_kernel(tc, x, w_words, w_scales, u_words, u_scales, out):
    nc = tc.nc
    with ExitStack() as ctx:
        sb = ctx.enter_context(tc.tile_pool(name="sb", bufs=1))
        ps = ctx.enter_context(tc.psum_pool(name="ps", bufs=1))
        ctx.enter_context(tc.manual_schedule())

        w_sb = sb.tile([P, 2 * M], U8, name="w_sb", align_bytes=64)
        u_sb = sb.tile([P, 2 * M], U8, name="u_sb", align_bytes=64)
        wscale = sb.tile([P, 2 * M], U8, name="wscale", align_bytes=64)
        codes = sb.tile([P, N], U32, name="codes", align_bytes=64)
        xscale = sb.tile([P, N], U8, name="xscale", align_bytes=64)

        nc.vector.memset(wscale[:].bitcast(I32), 0)

        x_rows = x.rearrange("g (p j) n -> (g p) j n", j=PACK)
        w_rows = w_scales.rearrange("g f m -> (g f) m").bitcast(I32)
        u_rows = u_scales.rearrange("g f m -> (g f) m").bitcast(I32)

        def load_scales(engine, rows, col0, quad):
            engine.dma_start(
                out=wscale[QUAD * quad : QUAD * quad + SCALE_ROWS, col0 : col0 + M].bitcast(I32),
                in_=rows[SCALE_ROWS * quad : SCALE_ROWS * (quad + 1), :],
            )

        raw = sb.tile([P, PACK, N], F32, name="raw")
        nc.sync.dma_start(out=raw[:, :PAIR, :], in_=x_rows[:, :PAIR, :])
        for quad in range(QUADS):
            load_scales((nc.sync, nc.scalar)[quad % 2], w_rows, 0, quad)
        nc.sync.dma_start(out=raw[:, PAIR:, :], in_=x_rows[:, PAIR:, :])
        for words, tile_sb in ((w_words, w_sb), (u_words, u_sb)):
            nc.sync.dma_start(out=tile_sb[:].bitcast(I32), in_=words.rearrange("g p b -> (g p) b").bitcast(I32))
        for quad in range(QUADS):
            load_scales(nc.sync, u_rows, M, quad)

        first = sb.tile([P, HALF, PACK], BF16, name="first", align_bytes=64)
        second = sb.tile([P, HALF, PACK], BF16, name="second", align_bytes=64)

        def walk(grouped, col0, lo, hi, places):
            src = raw[:, places, col0 + lo : col0 + hi].rearrange("p j (c i) -> p c j i", i=2)
            dst = grouped[:, lo:hi, places].rearrange("p (c i) j -> p c j i", i=2)
            return dst, src

        for places in (slice(0, PAIR), slice(PAIR, PACK)):
            dst, src = walk(second, HALF, VEC_COLS, HALF, places)
            nc.scalar.activation(out=dst, in_=src, func=ACT.Copy)
            dst, src = walk(first, 0, 0, HALF, places)
            nc.vector.tensor_copy(out=dst, in_=src)
            dst, src = walk(second, HALF, 0, VEC_COLS, places)
            nc.vector.tensor_copy(out=dst, in_=src)
        for c, grouped in enumerate((first, second)):
            cols = slice(c * HALF, (c + 1) * HALF)
            nc.vector.quantize_mx(
                out=codes[:, cols].bitcast(FP8X4),
                scales=xscale[:, cols],
                in_=grouped[:].rearrange("p n j -> p (n j)"),
            )

        sums = {}
        for name, words, col0 in (("h", w_sb, 0), ("u", u_sb, M)):
            for g in range(G):
                rows = slice(ROWS * g, ROWS * (g + 1))
                acc = ps.tile([M, N], F32, name="acc_%s%d" % (name, g))
                nc.tensor.matmul_mx(
                    out=acc[:],
                    lhsT=words[rows, :].bitcast(FP4X4),
                    lhsT_scale=wscale[rows, col0 : col0 + M],
                    rhs=codes[rows, :].bitcast(FP8X4),
                    rhs_scale=xscale[rows, :],
                    start=True,
                    stop=True,
                )
                sums[name, g] = acc

        for g in range(G):
            for h in range(2):
                cols = slice(h * HALF, (h + 1) * HALF)
                gate = sb.tile([M, HALF], F32, name="gate%d_%d" % (g, h))
                nc.scalar.activation(out=gate[:], in_=sums["h", g][:, cols], func=ACT.Tanh)
                result = sb.tile([M, HALF], F32, name="result%d_%d" % (g, h))
                nc.vector.tensor_tensor(out=result[:], in0=sums["u", g][:, cols], in1=gate[:], op=ALU.mult)
                nc.sync.dma_start(out=out[g][:, cols], in_=result[:])
